import numpy as np, ml_dtypes
CORES = [24,40,56,80,88,96]
N = 6
NB, TK, FT = 16, 128, 1
def setup_inputs(rng):
    return {"x": rng.standard_normal((N, NB, 128, TK), dtype=np.float32).astype(ml_dtypes.bfloat16), "w1": (rng.standard_normal((N, 128, FT * 128), dtype=np.float32) / 8).astype(ml_dtypes.bfloat16), "w2": (rng.standard_normal((N, 128, FT * 128), dtype=np.float32) / np.float32(8 * np.sqrt(FT))).astype(ml_dtypes.bfloat16)}
def setup_inputs_big(rng):
    d = setup_inputs(rng)
    for k in ("x",): d[k] = (d[k].astype(np.float32) * 1048576.0).astype(d[k].dtype)
    return d
def setup_inputs_small(rng):
    d = setup_inputs(rng)
    for k in ("x",): d[k] = (d[k].astype(np.float32) * (1 / 1048576.0)).astype(d[k].dtype)
    return d
def reference(x, w1, w2):
    W1, W2 = w1.astype(np.float64), w2.astype(np.float64)
    a = x[0].astype(np.float64)
    for s in range(N):
        a = sum(np.einsum("kf,bkn->bfn", W2[s][:, 128 * f:128 * f + 128], np.maximum(np.einsum("kf,bkn->bfn", W1[s][:, 128 * f:128 * f + 128], a), 0.0)) for f in range(FT))
    y = np.full(x.shape, np.nan, ml_dtypes.bfloat16)
    y[N - 1] = a.astype(ml_dtypes.bfloat16)
    return {"y": y}

@@ -1,0 +1,240 @@
+from concourse.bass import DstId, RemoteDMATransfer
+from concourse.mybir import AluOpType
+
+K = 4
+SKEW = 2
+BF = "bfloat16"
+SCRATCH = {
+    "xs": ("dram", [8, 128, 256], BF),
+    "ys": ("dram", [8, 128, 256], BF),
+    "w0": ("sbuf", [128, 384], BF),
+    "wb": ("sbuf", [128, 5 * 256], BF),
+    "xb": ("sbuf", [128, 512], BF),
+    "u0": ("sbuf", [128, 256], BF), "u1": ("sbuf", [128, 256], BF),
+    "v0": ("sbuf", [128, 256], BF), "v1": ("sbuf", [128, 256], BF),
+    "o0": ("sbuf", [128, 256], BF), "o1": ("sbuf", [128, 256], BF),
+    "zero": ("sbuf", [128, 256], BF),
+    "ps0": ("psum", [128, 512], "float32"), "ps1": ("psum", [128, 512], "float32"),
+    "pt0": ("psum", [128, 512], "float32"), "pt1": ("psum", [128, 512], "float32"),
+}
+SEMAPHORES = (["wl", "xl0", "xl1", "sent", "st", "wr", "w0a", "xa0", "xa1", "wq", "wp", "zr",
+               "mm0", "mm1", "vv0", "vv1"] + ["ws%d" % s for s in range(1, 6)] + ["ya%d" % c for c in range(8)])
+
+
+def _bits(mask):
+    return [1 << i for i in range(mask.bit_length()) if (mask >> i) & 1]
+
+
+def _split(mask, n):
+    es = _bits(mask)
+    per = len(es) // n
+    return [sum(es[i * per:(i + 1) * per]) for i in range(n)]
+
+
+def _first(mask, n):
+    return sum(_bits(mask)[:n])
+
+
+def rank_program(g, core, T, topo):
+    cores = list(T.cores)
+    n = len(cores)
+    src, snk = cores[0], cores[-1]
+    sem = T.sem
+    allc = range(topo.CORES_PER_CHIP * topo.CHIPS)
+
+    def on_chip(c):
+        return [d for d in allc if topo.chip(d) == topo.chip(c) and d != c]
+
+    def did(c):
+        rid, pid, _ = topo.addr(c)
+        return DstId(rid=rid, pnc=pid)
+
+    comp = [c for c in on_chip(src) if topo.may_write(c, snk) and c not in cores][:K]
+    direct = [s for s in range(1, n) if topo.may_write(cores[s], comp[0])]
+    scat = direct[-1]
+    relay = {}
+    relays_of = {}
+    for s in range(1, n):
+        if s not in direct:
+            rl = [c for c in on_chip(cores[s]) if topo.may_write(c, comp[0]) and c not in cores][:K]
+            relays_of[s] = rl
+            for i, c in enumerate(rl):
+                relay[c] = (s, i)
+
+    def wslot(s):
+        return T.wb[:, (s - 1) * 256:s * 256]
+
+    rank = T.rank_of(core)
+    sent = 0
+
+    if core == src:
+        g.sync.dma_start(T.w0[0:64, 0:256], T.w1[:, :]).then_inc(sem.wl, 16)
+        g.scalar.dma_start(T.w0[64:128, 0:256], T.w1[:, :]).then_inc(sem.wl, 16)
+        g.sync.dma_start(T.w0[:, 256:384], T.w2[:, :]).then_inc(sem.wl, 16)
+        g.scalar.dma_start(T.xs[0:4], T.x[0:8]).then_inc(sem.xl0, 16)
+        g.sync.dma_start(T.xs[4:8], T.x[8:16]).then_inc(sem.xl1, 16)
+        grp = _split(topo.mask(src, comp[0]), K)
+        ne = len(_bits(grp[0]))
+        g.wait_ge(sem.wl, 48)
+        g.remote_dma_fused([RemoteDMATransfer(dst_ids=[did(c)], dma_engine_mask=grp[j], remote_sem=sem.w0a,
+                                              src=T.w0[:, :], dst=T.w0[:, :]) for j, c in enumerate(comp)],
+                           local_sem=sem.sent)
+        sent += K * ne
+        for h in range(2):
+            g.wait_ge(sem["xl%d" % h], 16)
+            g.remote_dma_fused([RemoteDMATransfer(dst_ids=[did(c)], dma_engine_mask=grp[j],
+                                                  remote_sem=sem["xa%d" % h], src=T.xs[4 * h + j],
+                                                  dst=T.xb[:, h * 256:(h + 1) * 256]) for j, c in enumerate(comp)],
+                               local_sem=sem.sent)
+            sent += K * ne
+        g.wait_ge(sem.sent, sent)
+        return
+
+    if rank is not None:
+        s = rank
+        g.sync.dma_start(T.wb[:, (s - 1) * 256:(s - 1) * 256 + 128], T.w1[:, :]).then_inc(sem.wl, 16)
+        g.scalar.dma_start(T.wb[:, (s - 1) * 256 + 128:s * 256], T.w2[:, :]).then_inc(sem.wl, 16)
+        g.wait_ge(sem.wl, 32)
+        if s in direct:
+            grp = _split(topo.mask(core, comp[0]), K)
+            ne = len(_bits(grp[0]))
+            tr = []
+            for j, c in enumerate(comp):
+                if s == scat:
+                    a = (s - 1) * 256 + j * 64
+                    tr.append(RemoteDMATransfer(dst_ids=[did(c)], dma_engine_mask=grp[j], remote_sem=sem.wq,
+                                                src=T.wb[:, a:a + 64], dst=T.wb[:, a:a + 64]))
+                else:
+                    tr.append(RemoteDMATransfer(dst_ids=[did(c)], dma_engine_mask=grp[j],
+                                                remote_sem=sem["ws%d" % s], src=wslot(s), dst=wslot(s)))
+            g.remote_dma_fused(tr, local_sem=sem.sent)
+            sent += K * ne
+        else:
+            rl = relays_of[s]
+            m = _first(topo.mask(core, rl[0]), 8)
+            g.remote_dma_fused([RemoteDMATransfer(dst_ids=[did(c) for c in rl], dma_engine_mask=m,
+                                                  remote_sem=sem.wr, srcs=[wslot(s)],
+                                                  dsts=[wslot(s) for c in rl])], local_sem=sem.sent)
+            sent += 8
+        if core == snk:
+            ne = len(_bits(topo.mask(comp[0], snk)))
+            for h, q in ((0, g.sync), (1, g.scalar)):
+                for j in range(K):
+                    c = 4 * h + j
+                    q.wait_ge(sem["ya%d" % c], ne)
+                    q.dma_start(T.y[2 * c:2 * c + 2], T.ys[c]).then_inc(sem.st, 16)
+            g.wait_ge(sem.st, 16 * 8)
+        g.wait_ge(sem.sent, sent)
+        return
+
+    if core in relay:
+        s, i = relay[core]
+        rid, pid, _ = topo.addr(comp[i])
+        m = topo.mask(core, comp[i])
+        g.wait_ge(sem.wr, 8)
+        g.remote_dma(wslot(s), wslot(s), sem["ws%d" % s], sem.sent, pid, rid, m)
+        g.wait_ge(sem.sent, len(_bits(m)))
+        return
+
+    if core not in comp:
+        return
+
+    j = comp.index(core)
+    out_mask = topo.mask(core, snk)
+    n_out = len(_bits(out_mask))
+    peers = [c for c in comp if c != core]
+    nq = len(_bits(_split(topo.mask(cores[scat], core), K)[0]))
+    a = (scat - 1) * 256 + j * 64
+    g.wait_ge(sem.wq, nq)
+    g.remote_dma_fused([RemoteDMATransfer(dst_ids=[did(c) for c in peers], dma_engine_mask=out_mask,
+                                          remote_sem=sem.wp, srcs=[T.wb[:, a:a + 64]],
+                                          dsts=[T.wb[:, a:a + 64] for c in peers])], local_sem=sem.sent)
+    sent += n_out
+
+    te, ve = g.tensor, g.vector
+    ve.memset(T.zero[:, :], 0.0).then_inc(sem.zr, 1)
+    ve.wait_ge(sem.zr, 1)
+    n_x = len(_bits(_split(topo.mask(src, core), K)[0]))
+    ps = [T.ps0, T.ps1]
+    pt = [T.pt0, T.pt1]
+    u = [T.u0, T.u1]
+    v = [T.v0, T.v1]
+    o = [T.o0, T.o1]
+    mm = [sem.mm0, sem.mm1]
+    vv = [sem.vv0, sem.vv1]
+    nmm = [0, 0]
+    nvv = [0, 0]
+    seen = set()
+    P = 2 * n
+
+    def wait_weights(s):
+        if s in seen:
+            return
+        seen.add(s)
+        if s == 0:
+            te.wait_ge(sem.w0a, n_x)
+        elif s == scat:
+            te.wait_ge(sem.wq, nq)
+            te.wait_ge(sem.wp, n_out * len(peers))
+        elif s in direct:
+            te.wait_ge(sem["ws%d" % s], len(_bits(_split(topo.mask(cores[s], core), K)[0])))
+        else:
+            te.wait_ge(sem["ws%d" % s], len(_bits(topo.mask(relays_of[s][j], core))))
+
+    def do_pass(p, c):
+        s = p // 2
+        wait_weights(s)
+        if p == 0:
+            te.wait_ge(sem["xa%d" % c], n_x)
+            for b in range(2):
+                for e in range(2):
+                    te.matmul(out=(ps[c] if b == 0 else pt[c])[:, 0:128],
+                              lhsT=T.w0[b * 64:(b + 1) * 64, e * 128:(e + 1) * 128],
+                              rhs=T.xb[b * 64:(b + 1) * 64, c * 256 + e * 128:c * 256 + (e + 1) * 128],
+                              start=(e == 0), stop=(e == 1)).then_inc(mm[c], 1)
+                    nmm[c] += 1
+        else:
+            te.wait_ge(vv[c], nvv[c])
+            if p == 1:
+                w = T.w0[:, 256:384]
+            else:
+                w0c = (s - 1) * 256 + (p % 2) * 128
+                w = T.wb[:, w0c:w0c + 128]
+            rhs = u[c] if p % 2 else v[c]
+            if p < P - 1:
+                te.matmul(out=ps[c][:, 0:256], lhsT=w, rhs=rhs[:, :], start=True, stop=True).then_inc(mm[c], 1)
+                nmm[c] += 1
+            else:
+                for b in range(2):
+                    for e in range(2):
+                        te.matmul(out=ps[c][b * 64:(b + 1) * 64, e * 128:(e + 1) * 128],
+                                  lhsT=T.wb[:, w0c + e:w0c + 128:2], rhs=rhs[:, b * 128:(b + 1) * 128],
+                                  start=True, stop=True).then_inc(mm[c], 1)
+                        nmm[c] += 1
+        ve.wait_ge(mm[c], nmm[c])
+        nvv[c] += 1
+        if p == 0:
+            ve.tensor_tensor(out=u[c][:, 0:128], in0=ps[c][:, 0:128], in1=T.zero[:, 0:128],
+                             op=AluOpType.max).then_inc(vv[c], 1)
+            ve.tensor_tensor(out=u[c][:, 128:256], in0=pt[c][:, 0:128], in1=T.zero[:, 0:128],
+                             op=AluOpType.max).then_inc(vv[c], 1)
+            nvv[c] += 1
+        elif p % 2 == 0:
+            ve.tensor_tensor(out=u[c][:, :], in0=ps[c][:, 0:256], in1=T.zero[:, :],
+                             op=AluOpType.max).then_inc(vv[c], 1)
+        else:
+            dst = o[c] if p == P - 1 else v[c]
+            ve.tensor_copy(out=dst[:, :], in_=ps[c][:, 0:256]).then_inc(vv[c], 1)
+
+    for t in range(P + SKEW):
+        if t < P:
+            do_pass(t, 0)
+        if t >= SKEW:
+            do_pass(t - SKEW, 1)
+
+    rid, pid, _ = topo.addr(snk)
+    for c in range(2):
+        g.wait_ge(vv[c], nvv[c])
+        g.remote_dma(T.ys[4 * c + j], o[c][:, :], sem["ya%d" % (4 * c + j)], sem.sent, pid, rid, out_mask)
+        sent += n_out
+    g.wait_ge(sem.sent, sent)

@@ -2,8 +2,8 @@ from concourse.bass import DstId, RemoteDMATransfer
 from concourse.mybir import AluOpType
 
 K = 4
-SKEW = 2
 BF = "bfloat16"
+F32 = "float32"
 SCRATCH = {
     "xs": ("dram", [8, 128, 256], BF),
     "ys": ("dram", [8, 128, 256], BF),
@@ -13,12 +13,15 @@ SCRATCH = {
     "u0": ("sbuf", [128, 256], BF), "u1": ("sbuf", [128, 256], BF),
     "v0": ("sbuf", [128, 256], BF), "v1": ("sbuf", [128, 256], BF),
     "o0": ("sbuf", [128, 256], BF), "o1": ("sbuf", [128, 256], BF),
-    "zero": ("sbuf", [128, 256], BF),
-    "ps0": ("psum", [128, 512], "float32"), "ps1": ("psum", [128, 512], "float32"),
-    "pt0": ("psum", [128, 512], "float32"), "pt1": ("psum", [128, 512], "float32"),
+    "zero": ("sbuf", [128, 128], BF),
+    "ps00": ("psum", [128, 512], F32), "ps01": ("psum", [128, 512], F32),
+    "ps10": ("psum", [128, 512], F32), "ps11": ("psum", [128, 512], F32),
+    "pf0": ("psum", [128, 512], F32), "pf1": ("psum", [128, 512], F32),
 }
-SEMAPHORES = (["wl", "xl0", "xl1", "sent", "st", "wr", "w0a", "xa0", "xa1", "wq", "wp", "zr",
-               "mm0", "mm1", "vv0", "vv1"] + ["ws%d" % s for s in range(1, 6)] + ["ya%d" % c for c in range(8)])
+SEMAPHORES = (["wl", "xl0", "xl1", "sent", "st", "wr", "w0a", "xa0", "xa1", "zr", "mf0", "mf1", "vf0", "vf1"]
+              + ["%s%d%d" % (a, c, b) for a in ("mm", "vv") for c in range(2) for b in range(2)]
+              + ["%s%d" % (a, s) for s in range(1, 6) for a in ("ws", "wq", "wp")]
+              + ["ya%d" % c for c in range(8)])
 
 
 def _bits(mask):
@@ -51,12 +54,14 @@ def rank_program(g, core, T, topo):
 
     comp = [c for c in on_chip(src) if topo.may_write(c, snk) and c not in cores][:K]
     direct = [s for s in range(1, n) if topo.may_write(cores[s], comp[0])]
-    scat = direct[-1]
+    scat = direct[1:]
     relay = {}
     relays_of = {}
     for s in range(1, n):
         if s not in direct:
             rl = [c for c in on_chip(cores[s]) if topo.may_write(c, comp[0]) and c not in cores][:K]
+            if s == n - 1:
+                rl = [c for c in rl if topo.die(c) != topo.die(cores[direct[0]])]
             relays_of[s] = rl
             for i, c in enumerate(rl):
                 relay[c] = (s, i)
@@ -100,9 +105,10 @@ def rank_program(g, core, T, topo):
             ne = len(_bits(grp[0]))
             tr = []
             for j, c in enumerate(comp):
-                if s == scat:
+                if s in scat:
                     a = (s - 1) * 256 + j * 64
-                    tr.append(RemoteDMATransfer(dst_ids=[did(c)], dma_engine_mask=grp[j], remote_sem=sem.wq,
+                    tr.append(RemoteDMATransfer(dst_ids=[did(c)], dma_engine_mask=grp[j],
+                                                remote_sem=sem["wq%d" % s],
                                                 src=T.wb[:, a:a + 64], dst=T.wb[:, a:a + 64]))
                 else:
                     tr.append(RemoteDMATransfer(dst_ids=[did(c)], dma_engine_mask=grp[j],
@@ -118,9 +124,10 @@ def rank_program(g, core, T, topo):
             sent += 8
         if core == snk:
             ne = len(_bits(topo.mask(comp[0], snk)))
-            for h, q in ((0, g.sync), (1, g.scalar)):
+            for h in range(2):
                 for j in range(K):
                     c = 4 * h + j
+                    q = g.sync if j % 2 == 0 else g.scalar
                     q.wait_ge(sem["ya%d" % c], ne)
                     q.dma_start(T.y[2 * c:2 * c + 2], T.ys[c]).then_inc(sem.st, 16)
             g.wait_ge(sem.st, 16 * 8)
@@ -129,10 +136,12 @@ def rank_program(g, core, T, topo):
 
     if core in relay:
         s, i = relay[core]
-        rid, pid, _ = topo.addr(comp[i])
+        mine = comp[i::len(relays_of[s])]
         m = topo.mask(core, comp[i])
         g.wait_ge(sem.wr, 8)
-        g.remote_dma(wslot(s), wslot(s), sem["ws%d" % s], sem.sent, pid, rid, m)
+        g.remote_dma_fused([RemoteDMATransfer(dst_ids=[did(c) for c in mine], dma_engine_mask=m,
+                                              remote_sem=sem["ws%d" % s], srcs=[wslot(s)],
+                                              dsts=[wslot(s) for c in mine])], local_sem=sem.sent)
         g.wait_ge(sem.sent, len(_bits(m)))
         return
 
@@ -143,27 +152,26 @@ def rank_program(g, core, T, topo):
     out_mask = topo.mask(core, snk)
     n_out = len(_bits(out_mask))
     peers = [c for c in comp if c != core]
-    nq = len(_bits(_split(topo.mask(cores[scat], core), K)[0]))
-    a = (scat - 1) * 256 + j * 64
-    g.wait_ge(sem.wq, nq)
-    g.remote_dma_fused([RemoteDMATransfer(dst_ids=[did(c) for c in peers], dma_engine_mask=out_mask,
-                                          remote_sem=sem.wp, srcs=[T.wb[:, a:a + 64]],
-                                          dsts=[T.wb[:, a:a + 64] for c in peers])], local_sem=sem.sent)
-    sent += n_out
+    nq = len(_bits(_split(topo.mask(cores[scat[0]], core), K)[0]))
+    for s in scat:
+        a = (s - 1) * 256 + j * 64
+        g.wait_ge(sem["wq%d" % s], nq)
+        g.remote_dma_fused([RemoteDMATransfer(dst_ids=[did(c) for c in peers], dma_engine_mask=out_mask,
+                                              remote_sem=sem["wp%d" % s], srcs=[T.wb[:, a:a + 64]],
+                                              dsts=[T.wb[:, a:a + 64] for c in peers])], local_sem=sem.sent)
+        sent += n_out
 
     te, ve = g.tensor, g.vector
     ve.memset(T.zero[:, :], 0.0).then_inc(sem.zr, 1)
     ve.wait_ge(sem.zr, 1)
     n_x = len(_bits(_split(topo.mask(src, core), K)[0]))
-    ps = [T.ps0, T.ps1]
-    pt = [T.pt0, T.pt1]
+    ps = [[T.ps00, T.ps01], [T.ps10, T.ps11]]
+    pf = [T.pf0, T.pf1]
     u = [T.u0, T.u1]
     v = [T.v0, T.v1]
     o = [T.o0, T.o1]
-    mm = [sem.mm0, sem.mm1]
-    vv = [sem.vv0, sem.vv1]
-    nmm = [0, 0]
-    nvv = [0, 0]
+    nmm = {}
+    nvv = {}
     seen = set()
     P = 2 * n
 
@@ -173,68 +181,75 @@ def rank_program(g, core, T, topo):
         seen.add(s)
         if s == 0:
             te.wait_ge(sem.w0a, n_x)
-        elif s == scat:
-            te.wait_ge(sem.wq, nq)
-            te.wait_ge(sem.wp, n_out * len(peers))
+        elif s in scat:
+            te.wait_ge(sem["wq%d" % s], nq)
+            te.wait_ge(sem["wp%d" % s], n_out * len(peers))
         elif s in direct:
             te.wait_ge(sem["ws%d" % s], len(_bits(_split(topo.mask(cores[s], core), K)[0])))
         else:
-            te.wait_ge(sem["ws%d" % s], len(_bits(topo.mask(relays_of[s][j], core))))
+            te.wait_ge(sem["ws%d" % s], len(_bits(topo.mask(relays_of[s][j % len(relays_of[s])], core))))
 
-    def do_pass(p, c):
+    def do_pass(p, c, b):
         s = p // 2
+        k = (c, b)
+        mm, vv = sem["mm%d%d" % k], sem["vv%d%d" % k]
+        cols = slice(b * 128, (b + 1) * 128)
+        bank = ps[c][b][:, 0:128]
         wait_weights(s)
         if p == 0:
             te.wait_ge(sem["xa%d" % c], n_x)
-            for b in range(2):
-                for e in range(2):
-                    te.matmul(out=(ps[c] if b == 0 else pt[c])[:, 0:128],
-                              lhsT=T.w0[b * 64:(b + 1) * 64, e * 128:(e + 1) * 128],
-                              rhs=T.xb[b * 64:(b + 1) * 64, c * 256 + e * 128:c * 256 + (e + 1) * 128],
-                              start=(e == 0), stop=(e == 1)).then_inc(mm[c], 1)
-                    nmm[c] += 1
+            for e in range(2):
+                te.matmul(out=bank, lhsT=T.w0[b * 64:(b + 1) * 64, e * 128:(e + 1) * 128],
+                          rhs=T.xb[b * 64:(b + 1) * 64, c * 256 + e * 128:c * 256 + (e + 1) * 128],
+                          start=(e == 0), stop=(e == 1)).then_inc(mm, 1)
+            nmm[k] = 2
+            nvv[k] = 0
         else:
-            te.wait_ge(vv[c], nvv[c])
+            te.wait_ge(vv, nvv[k])
             if p == 1:
                 w = T.w0[:, 256:384]
             else:
                 w0c = (s - 1) * 256 + (p % 2) * 128
                 w = T.wb[:, w0c:w0c + 128]
             rhs = u[c] if p % 2 else v[c]
-            if p < P - 1:
-                te.matmul(out=ps[c][:, 0:256], lhsT=w, rhs=rhs[:, :], start=True, stop=True).then_inc(mm[c], 1)
-                nmm[c] += 1
-            else:
-                for b in range(2):
-                    for e in range(2):
-                        te.matmul(out=ps[c][b * 64:(b + 1) * 64, e * 128:(e + 1) * 128],
-                                  lhsT=T.wb[:, w0c + e:w0c + 128:2], rhs=rhs[:, b * 128:(b + 1) * 128],
-                                  start=True, stop=True).then_inc(mm[c], 1)
-                        nmm[c] += 1
-        ve.wait_ge(mm[c], nmm[c])
-        nvv[c] += 1
-        if p == 0:
-            ve.tensor_tensor(out=u[c][:, 0:128], in0=ps[c][:, 0:128], in1=T.zero[:, 0:128],
-                             op=AluOpType.max).then_inc(vv[c], 1)
-            ve.tensor_tensor(out=u[c][:, 128:256], in0=pt[c][:, 0:128], in1=T.zero[:, 0:128],
-                             op=AluOpType.max).then_inc(vv[c], 1)
-            nvv[c] += 1
-        elif p % 2 == 0:
-            ve.tensor_tensor(out=u[c][:, :], in0=ps[c][:, 0:256], in1=T.zero[:, :],
-                             op=AluOpType.max).then_inc(vv[c], 1)
+            te.matmul(out=bank, lhsT=w, rhs=rhs[:, cols], start=True, stop=True).then_inc(mm, 1)
+            nmm[k] += 1
+        ve.wait_ge(mm, nmm[k])
+        if p % 2 == 0:
+            ve.tensor_tensor(out=u[c][:, cols], in0=bank, in1=T.zero[:, :], op=AluOpType.max).then_inc(vv, 1)
         else:
-            dst = o[c] if p == P - 1 else v[c]
-            ve.tensor_copy(out=dst[:, :], in_=ps[c][:, 0:256]).then_inc(vv[c], 1)
+            ve.tensor_copy(out=v[c][:, cols], in_=bank).then_inc(vv, 1)
+        nvv[k] += 1
 
-    for t in range(P + SKEW):
-        if t < P:
-            do_pass(t, 0)
-        if t >= SKEW:
-            do_pass(t - SKEW, 1)
+    def do_last(c):
+        w0c = (n - 2) * 256 + 128
+        for b in range(2):
+            te.wait_ge(sem["vv%d%d" % (c, b)], nvv[(c, b)])
+            for e in range(2):
+                te.matmul(out=pf[c][b * 64:(b + 1) * 64, e * 128:(e + 1) * 128],
+                          lhsT=T.wb[:, w0c + e:w0c + 128:2], rhs=u[c][:, b * 128:(b + 1) * 128],
+                          start=True, stop=True).then_inc(sem["mf%d" % c], 1)
+        ve.wait_ge(sem["mf%d" % c], 4)
+        ve.tensor_copy(out=o[c][:, :], in_=pf[c][:, 0:256]).then_inc(sem["vf%d" % c], 1)
+
+    together = 2 * min(relays_of) + 2
+    for c in range(2):
+        for p in range(2):
+            for b in range(2):
+                do_pass(p, c, b)
+    for p in range(2, together):
+        for c in range(2):
+            for b in range(2):
+                do_pass(p, c, b)
+    for c in range(2):
+        for p in range(together, P - 1):
+            for b in range(2):
+                do_pass(p, c, b)
+        do_last(c)
 
     rid, pid, _ = topo.addr(snk)
     for c in range(2):
-        g.wait_ge(vv[c], nvv[c])
+        g.wait_ge(sem["vf%d" % c], 1)
         g.remote_dma(T.ys[4 * c + j], o[c][:, :], sem["ya%d" % (4 * c + j)], sem.sent, pid, rid, out_mask)
         sent += n_out
     g.wait_ge(sem.sent, sent)

@@ -7,8 +7,12 @@ F32 = "float32"
 SCRATCH = {
     "xs": ("dram", [8, 128, 256], BF),
     "ys": ("dram", [8, 128, 256], BF),
+    "idd": ("dram", [129, 128], BF),
     "w0": ("sbuf", [128, 384], BF),
     "wb": ("sbuf", [128, 5 * 256], BF),
+    "tb": ("sbuf", [128, 5 * 128], BF),
+    "pb": ("sbuf", [128, 5 * 128], BF),
+    "zi": ("sbuf", [128, 129], BF), "ident": ("sbuf", [128, 128], BF),
     "xb": ("sbuf", [128, 512], BF),
     "u0": ("sbuf", [128, 256], BF), "u1": ("sbuf", [128, 256], BF),
     "v0": ("sbuf", [128, 256], BF), "v1": ("sbuf", [128, 256], BF),
@@ -17,10 +21,13 @@ SCRATCH = {
     "ps00": ("psum", [128, 512], F32), "ps01": ("psum", [128, 512], F32),
     "ps10": ("psum", [128, 512], F32), "ps11": ("psum", [128, 512], F32),
     "pf0": ("psum", [128, 512], F32), "pf1": ("psum", [128, 512], F32),
+    "pw0": ("psum", [128, 512], F32), "pw1": ("psum", [128, 512], F32),
 }
-SEMAPHORES = (["wl", "xl0", "xl1", "sent", "st", "wr", "w0a", "xa0", "xa1", "zr", "mf0", "mf1", "vf0", "vf1"]
+SEMAPHORES = (["wl", "xl0", "xl1", "sent", "st", "wr", "w0a", "xa0", "xa1", "zr", "zs", "id1", "id2",
+               "mf0", "mf1", "vf0", "vf1"]
               + ["%s%d%d" % (a, c, b) for a in ("mm", "vv") for c in range(2) for b in range(2)]
               + ["%s%d" % (a, s) for s in range(1, 6) for a in ("ws", "wq", "wp")]
+              + ["%s%d" % (a, s) for s in range(5) for a in ("mt", "vt", "mp", "vp")]
               + ["ya%d" % c for c in range(8)])
 
 
@@ -32,10 +39,6 @@ def _split(mask, n):
     es = _bits(mask)
     per = len(es) // n
     return [sum(es[i * per:(i + 1) * per]) for i in range(n)]
-
-
-def _first(mask, n):
-    return sum(_bits(mask)[:n])
 
 
 def rank_program(g, core, T, topo):
@@ -117,11 +120,11 @@ def rank_program(g, core, T, topo):
             sent += K * ne
         else:
             rl = relays_of[s]
-            m = _first(topo.mask(core, rl[0]), 8)
+            m = topo.mask(core, rl[0])
             g.remote_dma_fused([RemoteDMATransfer(dst_ids=[did(c) for c in rl], dma_engine_mask=m,
                                                   remote_sem=sem.wr, srcs=[wslot(s)],
                                                   dsts=[wslot(s) for c in rl])], local_sem=sem.sent)
-            sent += 8
+            sent += len(_bits(m))
         if core == snk:
             ne = len(_bits(topo.mask(comp[0], snk)))
             for h in range(2):
@@ -138,7 +141,7 @@ def rank_program(g, core, T, topo):
         s, i = relay[core]
         mine = comp[i::len(relays_of[s])]
         m = topo.mask(core, comp[i])
-        g.wait_ge(sem.wr, 8)
+        g.wait_ge(sem.wr, len(_bits(topo.mask(cores[s], core))))
         g.remote_dma_fused([RemoteDMATransfer(dst_ids=[did(c) for c in mine], dma_engine_mask=m,
                                               remote_sem=sem["ws%d" % s], srcs=[wslot(s)],
                                               dsts=[wslot(s) for c in mine])], local_sem=sem.sent)
@@ -152,6 +155,19 @@ def rank_program(g, core, T, topo):
     out_mask = topo.mask(core, snk)
     n_out = len(_bits(out_mask))
     peers = [c for c in comp if c != core]
+    te, ve = g.tensor, g.vector
+
+    ve.memset(T.zi[:, :], 0.0).then_inc(sem.zs, 1)
+    ve.wait_ge(sem.zs, 1)
+    ve.memset(T.zi[:, 0:1], 1.0).then_inc(sem.zs, 1)
+    ve.memset(T.zero[:, :], 0.0).then_inc(sem.zr, 1)
+    ve.wait_ge(sem.zr, 1)
+    g.sync.wait_ge(sem.zs, 2)
+    g.sync.dma_start(T.idd[:, :], T.zi[:, :]).then_inc(sem.id1, 16)
+    g.sync.wait_ge(sem.id1, 16)
+    g.sync.dma_start(T.ident[:, :], T.idd[0:128, :]).then_inc(sem.id2, 16)
+    te.wait_ge(sem.id2, 16)
+
     nq = len(_bits(_split(topo.mask(cores[scat[0]], core), K)[0]))
     for s in scat:
         a = (s - 1) * 256 + j * 64
@@ -161,9 +177,6 @@ def rank_program(g, core, T, topo):
                                               dsts=[T.wb[:, a:a + 64] for c in peers])], local_sem=sem.sent)
         sent += n_out
 
-    te, ve = g.tensor, g.vector
-    ve.memset(T.zero[:, :], 0.0).then_inc(sem.zr, 1)
-    ve.wait_ge(sem.zr, 1)
     n_x = len(_bits(_split(topo.mask(src, core), K)[0]))
     ps = [[T.ps00, T.ps01], [T.ps10, T.ps11]]
     pf = [T.pf0, T.pf1]
@@ -173,7 +186,6 @@ def rank_program(g, core, T, topo):
     nmm = {}
     nvv = {}
     seen = set()
-    P = 2 * n
 
     def wait_weights(s):
         if s in seen:
@@ -189,14 +201,34 @@ def rank_program(g, core, T, topo):
         else:
             te.wait_ge(sem["ws%d" % s], len(_bits(topo.mask(relays_of[s][j % len(relays_of[s])], core))))
 
-    def do_pass(p, c, b):
-        s = p // 2
+    def blk(t, s):
+        return t[:, s * 128:(s + 1) * 128]
+
+    def mm_t(s):
+        wait_weights(s)
+        w2 = T.w0[:, 256:384] if s == 0 else T.wb[:, (s - 1) * 256 + 128:s * 256]
+        te.matmul(out=T.pw1[:, 0:128], lhsT=w2, rhs=T.ident[:, :], start=True, stop=True).then_inc(sem["mt%d" % s], 1)
+
+    def ev_t(s):
+        ve.wait_ge(sem["mt%d" % s], 1)
+        ve.tensor_copy(out=blk(T.tb, s), in_=T.pw1[:, 0:128]).then_inc(sem["vt%d" % s], 1)
+
+    def mm_p(s):
+        wait_weights(s + 1)
+        te.wait_ge(sem["vt%d" % s], 1)
+        te.matmul(out=T.pw0[:, 0:128], lhsT=blk(T.tb, s), rhs=T.wb[:, s * 256:s * 256 + 128],
+                  start=True, stop=True).then_inc(sem["mp%d" % s], 1)
+
+    def ev_p(s):
+        ve.wait_ge(sem["mp%d" % s], 1)
+        ve.tensor_copy(out=blk(T.pb, s), in_=T.pw0[:, 0:128]).then_inc(sem["vp%d" % s], 1)
+
+    def do_pass(q, c, b):
         k = (c, b)
         mm, vv = sem["mm%d%d" % k], sem["vv%d%d" % k]
-        cols = slice(b * 128, (b + 1) * 128)
         bank = ps[c][b][:, 0:128]
-        wait_weights(s)
-        if p == 0:
+        if q == 0:
+            wait_weights(0)
             te.wait_ge(sem["xa%d" % c], n_x)
             for e in range(2):
                 te.matmul(out=bank, lhsT=T.w0[b * 64:(b + 1) * 64, e * 128:(e + 1) * 128],
@@ -206,45 +238,44 @@ def rank_program(g, core, T, topo):
             nvv[k] = 0
         else:
             te.wait_ge(vv, nvv[k])
-            if p == 1:
-                w = T.w0[:, 256:384]
-            else:
-                w0c = (s - 1) * 256 + (p % 2) * 128
-                w = T.wb[:, w0c:w0c + 128]
-            rhs = u[c] if p % 2 else v[c]
-            te.matmul(out=bank, lhsT=w, rhs=rhs[:, cols], start=True, stop=True).then_inc(mm, 1)
+            te.wait_ge(sem["vp%d" % (q - 1)], 1)
+            te.matmul(out=bank, lhsT=blk(T.pb, q - 1), rhs=blk(u[c] if q % 2 else v[c], b),
+                      start=True, stop=True).then_inc(mm, 1)
             nmm[k] += 1
         ve.wait_ge(mm, nmm[k])
-        if p % 2 == 0:
-            ve.tensor_tensor(out=u[c][:, cols], in0=bank, in1=T.zero[:, :], op=AluOpType.max).then_inc(vv, 1)
-        else:
-            ve.tensor_copy(out=v[c][:, cols], in_=bank).then_inc(vv, 1)
+        ve.tensor_tensor(out=blk(v[c] if q % 2 else u[c], b), in0=bank, in1=T.zero[:, :],
+                         op=AluOpType.max).then_inc(vv, 1)
         nvv[k] += 1
 
     def do_last(c):
         w0c = (n - 2) * 256 + 128
+        h = u[c] if n % 2 else v[c]
         for b in range(2):
             te.wait_ge(sem["vv%d%d" % (c, b)], nvv[(c, b)])
             for e in range(2):
                 te.matmul(out=pf[c][b * 64:(b + 1) * 64, e * 128:(e + 1) * 128],
-                          lhsT=T.wb[:, w0c + e:w0c + 128:2], rhs=u[c][:, b * 128:(b + 1) * 128],
+                          lhsT=T.wb[:, w0c + e:w0c + 128:2], rhs=blk(h, b),
                           start=True, stop=True).then_inc(sem["mf%d" % c], 1)
         ve.wait_ge(sem["mf%d" % c], 4)
         ve.tensor_copy(out=o[c][:, :], in_=pf[c][:, 0:256]).then_inc(sem["vf%d" % c], 1)
 
-    together = 2 * min(relays_of) + 2
+    streams = [(c, b) for c in range(2) for b in range(2)]
+    mm_t(0)
+    ev_t(0)
+    for c, b in streams:
+        do_pass(0, c, b)
+    for q in range(1, n):
+        mm_p(q - 1)
+        if q < n - 1:
+            mm_t(q)
+        ev_p(q - 1)
+        if q < n - 1:
+            ev_t(q)
+            for c, b in streams:
+                do_pass(q, c, b)
     for c in range(2):
-        for p in range(2):
-            for b in range(2):
-                do_pass(p, c, b)
-    for p in range(2, together):
-        for c in range(2):
-            for b in range(2):
-                do_pass(p, c, b)
-    for c in range(2):
-        for p in range(together, P - 1):
-            for b in range(2):
-                do_pass(p, c, b)
+        for b in range(2):
+            do_pass(n - 1, c, b)
         do_last(c)
 
     rid, pid, _ = topo.addr(snk)

@@ -7,12 +7,12 @@ F32 = "float32"
 SCRATCH = {
     "xs": ("dram", [8, 128, 256], BF),
     "ys": ("dram", [8, 128, 256], BF),
-    "idd": ("dram", [129, 128], BF),
     "w0": ("sbuf", [128, 384], BF),
     "wb": ("sbuf", [128, 5 * 256], BF),
-    "tb": ("sbuf", [128, 5 * 128], BF),
+    "w2r": ("sbuf", [128, 128], BF),
+    "tb": ("sbuf", [128, 128], BF),
     "pb": ("sbuf", [128, 5 * 128], BF),
-    "zi": ("sbuf", [128, 129], BF), "ident": ("sbuf", [128, 128], BF),
+    "ones": ("sbuf", [128, 128], BF), "ident": ("sbuf", [128, 128], BF),
     "xb": ("sbuf", [128, 512], BF),
     "u0": ("sbuf", [128, 256], BF), "u1": ("sbuf", [128, 256], BF),
     "v0": ("sbuf", [128, 256], BF), "v1": ("sbuf", [128, 256], BF),
@@ -23,11 +23,11 @@ SCRATCH = {
     "pf0": ("psum", [128, 512], F32), "pf1": ("psum", [128, 512], F32),
     "pw0": ("psum", [128, 512], F32), "pw1": ("psum", [128, 512], F32),
 }
-SEMAPHORES = (["wl", "xl0", "xl1", "sent", "st", "wr", "w0a", "xa0", "xa1", "zr", "zs", "id1", "id2",
-               "mf0", "mf1", "vf0", "vf1"]
+SEMAPHORES = (["wl", "wl2", "xl0", "xl1", "sent", "st", "wr0", "wr1", "wn", "w0a", "xa0", "xa1", "zr", "zs", "idn",
+               "mt", "vt", "mf0", "mf1", "vf0", "vf1"]
               + ["%s%d%d" % (a, c, b) for a in ("mm", "vv") for c in range(2) for b in range(2)]
-              + ["%s%d" % (a, s) for s in range(1, 6) for a in ("ws", "wq", "wp")]
-              + ["%s%d" % (a, s) for s in range(5) for a in ("mt", "vt", "mp", "vp")]
+              + ["%s%d" % (a, s) for s in range(1, 6) for a in ("ws", "wt", "wq", "wx", "wp", "wy")]
+              + ["%s%d" % (a, s) for s in range(5) for a in ("mp", "vp")]
               + ["ya%d" % c for c in range(8)])
 
 
@@ -46,6 +46,7 @@ def rank_program(g, core, T, topo):
     n = len(cores)
     src, snk = cores[0], cores[-1]
     sem = T.sem
+    te, ve = g.tensor, g.vector
     allc = range(topo.CORES_PER_CHIP * topo.CHIPS)
 
     def on_chip(c):
@@ -57,7 +58,10 @@ def rank_program(g, core, T, topo):
 
     comp = [c for c in on_chip(src) if topo.may_write(c, snk) and c not in cores][:K]
     direct = [s for s in range(1, n) if topo.may_write(cores[s], comp[0])]
+    first = direct[0]
     scat = direct[1:]
+    nxt = first + 1
+    waves = [(s, p) for s in scat for p in range(2) if (s, p) != (nxt, 0)]
     relay = {}
     relays_of = {}
     for s in range(1, n):
@@ -69,8 +73,19 @@ def rank_program(g, core, T, topo):
             for i, c in enumerate(rl):
                 relay[c] = (s, i)
 
-    def wslot(s):
-        return T.wb[:, (s - 1) * 256:s * 256]
+    def blk(t, s):
+        return t[:, s * 128:(s + 1) * 128]
+
+    def quarter(s, part, j):
+        return ((s - 1) * 256 + part * 128 + j * (128 // K), 128 // K,
+                sem["%s%d" % (("wq", "wx")[part], s)], sem["%s%d" % (("wp", "wy")[part], s)])
+
+    def make_identity():
+        ve.memset(T.ones[:, :], 1.0).then_inc(sem.zs, 1)
+        g.wait_ge(sem.zs, 1)
+        g.affine_select(out=T.ident[:, :], in_=T.ones[:, :], pattern=[[-1, 128]], compare_op=AluOpType.is_equal,
+                        fill=0.0, base=0, channel_multiplier=1).then_inc(sem.idn, 1)
+        te.wait_ge(sem.idn, 1)
 
     rank = T.rank_of(core)
     sent = 0
@@ -81,8 +96,18 @@ def rank_program(g, core, T, topo):
         g.sync.dma_start(T.w0[:, 256:384], T.w2[:, :]).then_inc(sem.wl, 16)
         g.scalar.dma_start(T.xs[0:4], T.x[0:8]).then_inc(sem.xl0, 16)
         g.sync.dma_start(T.xs[4:8], T.x[8:16]).then_inc(sem.xl1, 16)
-        grp = _split(topo.mask(src, comp[0]), K)
-        ne = len(_bits(grp[0]))
+        es = _bits(topo.mask(src, comp[0]))
+        near = [c for c in comp if topo.die(c) == topo.die(src)]
+        far = [c for c in comp if topo.die(c) != topo.die(src)]
+        ne = len(es) // K
+        if len(near) == len(far):
+            grp_of = {}
+            for lst, mine in ((near, es[0::2]), (far, es[1::2])):
+                for i, c in enumerate(lst):
+                    grp_of[c] = sum(mine[i * ne:(i + 1) * ne])
+            grp = [grp_of[c] for c in comp]
+        else:
+            grp = _split(topo.mask(src, comp[0]), K)
         g.wait_ge(sem.wl, 48)
         g.remote_dma_fused([RemoteDMATransfer(dst_ids=[did(c)], dma_engine_mask=grp[j], remote_sem=sem.w0a,
                                               src=T.w0[:, :], dst=T.w0[:, :]) for j, c in enumerate(comp)],
@@ -100,31 +125,62 @@ def rank_program(g, core, T, topo):
 
     if rank is not None:
         s = rank
-        g.sync.dma_start(T.wb[:, (s - 1) * 256:(s - 1) * 256 + 128], T.w1[:, :]).then_inc(sem.wl, 16)
-        g.scalar.dma_start(T.wb[:, (s - 1) * 256 + 128:s * 256], T.w2[:, :]).then_inc(sem.wl, 16)
-        g.wait_ge(sem.wl, 32)
-        if s in direct:
-            grp = _split(topo.mask(core, comp[0]), K)
-            ne = len(_bits(grp[0]))
-            tr = []
-            for j, c in enumerate(comp):
-                if s in scat:
-                    a = (s - 1) * 256 + j * 64
-                    tr.append(RemoteDMATransfer(dst_ids=[did(c)], dma_engine_mask=grp[j],
-                                                remote_sem=sem["wq%d" % s],
-                                                src=T.wb[:, a:a + 64], dst=T.wb[:, a:a + 64]))
-                else:
-                    tr.append(RemoteDMATransfer(dst_ids=[did(c)], dma_engine_mask=grp[j],
-                                                remote_sem=sem["ws%d" % s], src=wslot(s), dst=wslot(s)))
-            g.remote_dma_fused(tr, local_sem=sem.sent)
-            sent += K * ne
+        a0 = (s - 1) * 256
+        turned = s < n - 1
+        g.sync.dma_start(T.wb[:, a0:a0 + 128], T.w1[:, :]).then_inc(sem.wl, 16)
+        if turned:
+            g.scalar.dma_start(T.w2r[:, :], T.w2[:, :]).then_inc(sem.wl2, 16)
+            make_identity()
+            te.wait_ge(sem.wl2, 16)
+            te.matmul(out=T.pw1[:, 0:128], lhsT=T.w2r[:, :], rhs=T.ident[:, :],
+                      start=True, stop=True).then_inc(sem.mt, 1)
+            ve.wait_ge(sem.mt, 1)
+            ve.tensor_copy(out=T.wb[:, a0 + 128:a0 + 256], in_=T.pw1[:, 0:128]).then_inc(sem.vt, 1)
         else:
-            rl = relays_of[s]
-            m = topo.mask(core, rl[0])
-            g.remote_dma_fused([RemoteDMATransfer(dst_ids=[did(c) for c in rl], dma_engine_mask=m,
-                                                  remote_sem=sem.wr, srcs=[wslot(s)],
-                                                  dsts=[wslot(s) for c in rl])], local_sem=sem.sent)
-            sent += len(_bits(m))
+            g.scalar.dma_start(T.wb[:, a0 + 128:a0 + 256], T.w2[:, :]).then_inc(sem.wl2, 16)
+        if s == first:
+            te.wait_ge(sem.vt, 1)
+            te.wait_ge(sem.wn, len(_bits(topo.mask(cores[nxt], core))))
+            te.matmul(out=T.pw0[:, 0:128], lhsT=T.wb[:, a0 + 128:a0 + 256], rhs=T.wb[:, s * 256:s * 256 + 128],
+                      start=True, stop=True).then_inc(sem["mp%d" % s], 1)
+            ve.wait_ge(sem["mp%d" % s], 1)
+            ve.tensor_copy(out=blk(T.pb, s), in_=T.pw0[:, 0:128]).then_inc(sem["vp%d" % s], 1)
+        g.wait_ge(sem.wl, 16)
+        for part in range(2):
+            a = a0 + part * 128
+            if part == 1:
+                if s == first:
+                    g.wait_ge(sem["vp%d" % s], 1)
+                elif turned:
+                    g.wait_ge(sem.vt, 1)
+                else:
+                    g.wait_ge(sem.wl2, 16)
+            if (s, part) == (nxt, 0):
+                m = topo.mask(core, cores[first])
+                rid, pid, _ = topo.addr(cores[first])
+                g.remote_dma(T.wb[:, a:a + 128], T.wb[:, a:a + 128], sem.wn, sem.sent, pid, rid, m)
+                sent += len(_bits(m))
+            elif s in direct:
+                grp = _split(topo.mask(core, comp[0]), K)
+                tr = []
+                for j, c in enumerate(comp):
+                    if s != first:
+                        b, wd, rs, _ = quarter(s, part, j)
+                        ap = T.wb[:, b:b + wd]
+                    else:
+                        rs = sem["%s%d" % (("ws", "wt")[part], s)]
+                        ap = T.wb[:, a:a + 128] if part == 0 else blk(T.pb, s)
+                    tr.append(RemoteDMATransfer(dst_ids=[did(c)], dma_engine_mask=grp[j], remote_sem=rs,
+                                                src=ap, dst=ap))
+                g.remote_dma_fused(tr, local_sem=sem.sent)
+                sent += K * len(_bits(grp[0]))
+            else:
+                rl = relays_of[s]
+                m = topo.mask(core, rl[0])
+                g.remote_dma_fused([RemoteDMATransfer(dst_ids=[did(c) for c in rl], dma_engine_mask=m,
+                                                      remote_sem=sem["wr%d" % part], srcs=[T.wb[:, a:a + 128]],
+                                                      dsts=[T.wb[:, a:a + 128] for c in rl])], local_sem=sem.sent)
+                sent += len(_bits(m))
         if core == snk:
             ne = len(_bits(topo.mask(comp[0], snk)))
             for h in range(2):
@@ -141,11 +197,13 @@ def rank_program(g, core, T, topo):
         s, i = relay[core]
         mine = comp[i::len(relays_of[s])]
         m = topo.mask(core, comp[i])
-        g.wait_ge(sem.wr, len(_bits(topo.mask(cores[s], core))))
-        g.remote_dma_fused([RemoteDMATransfer(dst_ids=[did(c) for c in mine], dma_engine_mask=m,
-                                              remote_sem=sem["ws%d" % s], srcs=[wslot(s)],
-                                              dsts=[wslot(s) for c in mine])], local_sem=sem.sent)
-        g.wait_ge(sem.sent, len(_bits(m)))
+        for part, nm in enumerate(("ws", "wt")):
+            a = (s - 1) * 256 + part * 128
+            g.wait_ge(sem["wr%d" % part], len(_bits(topo.mask(cores[s], core))))
+            g.remote_dma_fused([RemoteDMATransfer(dst_ids=[did(c) for c in mine], dma_engine_mask=m,
+                                                  remote_sem=sem["%s%d" % (nm, s)], srcs=[T.wb[:, a:a + 128]],
+                                                  dsts=[T.wb[:, a:a + 128] for c in mine])], local_sem=sem.sent)
+        g.wait_ge(sem.sent, 2 * len(_bits(m)))
         return
 
     if core not in comp:
@@ -155,29 +213,21 @@ def rank_program(g, core, T, topo):
     out_mask = topo.mask(core, snk)
     n_out = len(_bits(out_mask))
     peers = [c for c in comp if c != core]
-    te, ve = g.tensor, g.vector
 
-    ve.memset(T.zi[:, :], 0.0).then_inc(sem.zs, 1)
-    ve.wait_ge(sem.zs, 1)
-    ve.memset(T.zi[:, 0:1], 1.0).then_inc(sem.zs, 1)
+    make_identity()
     ve.memset(T.zero[:, :], 0.0).then_inc(sem.zr, 1)
     ve.wait_ge(sem.zr, 1)
-    g.sync.wait_ge(sem.zs, 2)
-    g.sync.dma_start(T.idd[:, :], T.zi[:, :]).then_inc(sem.id1, 16)
-    g.sync.wait_ge(sem.id1, 16)
-    g.sync.dma_start(T.ident[:, :], T.idd[0:128, :]).then_inc(sem.id2, 16)
-    te.wait_ge(sem.id2, 16)
 
     nq = len(_bits(_split(topo.mask(cores[scat[0]], core), K)[0]))
-    for s in scat:
-        a = (s - 1) * 256 + j * 64
-        g.wait_ge(sem["wq%d" % s], nq)
+    for s, part in waves:
+        a, wd, s_in, s_on = quarter(s, part, j)
+        g.wait_ge(s_in, nq)
         g.remote_dma_fused([RemoteDMATransfer(dst_ids=[did(c) for c in peers], dma_engine_mask=out_mask,
-                                              remote_sem=sem["wp%d" % s], srcs=[T.wb[:, a:a + 64]],
-                                              dsts=[T.wb[:, a:a + 64] for c in peers])], local_sem=sem.sent)
+                                              remote_sem=s_on, srcs=[T.wb[:, a:a + wd]],
+                                              dsts=[T.wb[:, a:a + wd] for c in peers])], local_sem=sem.sent)
         sent += n_out
 
-    n_x = len(_bits(_split(topo.mask(src, core), K)[0]))
+    n_x = len(_bits(topo.mask(src, core))) // K
     ps = [[T.ps00, T.ps01], [T.ps10, T.ps11]]
     pf = [T.pf0, T.pf1]
     u = [T.u0, T.u1]
@@ -187,39 +237,30 @@ def rank_program(g, core, T, topo):
     nvv = {}
     seen = set()
 
-    def wait_weights(s):
-        if s in seen:
+    def wait_weights(s, part):
+        key = (s, part) if s else s
+        if key in seen:
             return
-        seen.add(s)
+        seen.add(key)
         if s == 0:
             te.wait_ge(sem.w0a, n_x)
-        elif s in scat:
-            te.wait_ge(sem["wq%d" % s], nq)
-            te.wait_ge(sem["wp%d" % s], n_out * len(peers))
+        elif key in waves:
+            _, _, s_in, s_on = quarter(s, part, j)
+            te.wait_ge(s_in, nq)
+            te.wait_ge(s_on, n_out * len(peers))
         elif s in direct:
-            te.wait_ge(sem["ws%d" % s], len(_bits(_split(topo.mask(cores[s], core), K)[0])))
+            te.wait_ge(sem["%s%d" % (("ws", "wt")[part], s)], len(_bits(_split(topo.mask(cores[s], core), K)[0])))
         else:
-            te.wait_ge(sem["ws%d" % s], len(_bits(topo.mask(relays_of[s][j % len(relays_of[s])], core))))
+            te.wait_ge(sem["%s%d" % (("ws", "wt")[part], s)],
+                       len(_bits(topo.mask(relays_of[s][j % len(relays_of[s])], core))))
 
-    def blk(t, s):
-        return t[:, s * 128:(s + 1) * 128]
-
-    def mm_t(s):
-        wait_weights(s)
-        w2 = T.w0[:, 256:384] if s == 0 else T.wb[:, (s - 1) * 256 + 128:s * 256]
-        te.matmul(out=T.pw1[:, 0:128], lhsT=w2, rhs=T.ident[:, :], start=True, stop=True).then_inc(sem["mt%d" % s], 1)
-
-    def ev_t(s):
-        ve.wait_ge(sem["mt%d" % s], 1)
-        ve.tensor_copy(out=blk(T.tb, s), in_=T.pw1[:, 0:128]).then_inc(sem["vt%d" % s], 1)
-
-    def mm_p(s):
-        wait_weights(s + 1)
-        te.wait_ge(sem["vt%d" % s], 1)
-        te.matmul(out=T.pw0[:, 0:128], lhsT=blk(T.tb, s), rhs=T.wb[:, s * 256:s * 256 + 128],
-                  start=True, stop=True).then_inc(sem["mp%d" % s], 1)
-
-    def ev_p(s):
+    def do_p(s):
+        wait_weights(s, 1)
+        wait_weights(s + 1, 0)
+        if s == 0:
+            te.wait_ge(sem.vt, 1)
+        te.matmul(out=T.pw0[:, 0:128], lhsT=T.tb[:, :] if s == 0 else T.wb[:, (s - 1) * 256 + 128:s * 256],
+                  rhs=T.wb[:, s * 256:s * 256 + 128], start=True, stop=True).then_inc(sem["mp%d" % s], 1)
         ve.wait_ge(sem["mp%d" % s], 1)
         ve.tensor_copy(out=blk(T.pb, s), in_=T.pw0[:, 0:128]).then_inc(sem["vp%d" % s], 1)
 
@@ -228,7 +269,7 @@ def rank_program(g, core, T, topo):
         mm, vv = sem["mm%d%d" % k], sem["vv%d%d" % k]
         bank = ps[c][b][:, 0:128]
         if q == 0:
-            wait_weights(0)
+            wait_weights(0, 0)
             te.wait_ge(sem["xa%d" % c], n_x)
             for e in range(2):
                 te.matmul(out=bank, lhsT=T.w0[b * 64:(b + 1) * 64, e * 128:(e + 1) * 128],
@@ -238,7 +279,10 @@ def rank_program(g, core, T, topo):
             nvv[k] = 0
         else:
             te.wait_ge(vv, nvv[k])
-            te.wait_ge(sem["vp%d" % (q - 1)], 1)
+            if q - 1 == first:
+                wait_weights(first, 1)
+            else:
+                te.wait_ge(sem["vp%d" % (q - 1)], 1)
             te.matmul(out=bank, lhsT=blk(T.pb, q - 1), rhs=blk(u[c] if q % 2 else v[c], b),
                       start=True, stop=True).then_inc(mm, 1)
             nmm[k] += 1
@@ -250,6 +294,7 @@ def rank_program(g, core, T, topo):
     def do_last(c):
         w0c = (n - 2) * 256 + 128
         h = u[c] if n % 2 else v[c]
+        wait_weights(n - 1, 1)
         for b in range(2):
             te.wait_ge(sem["vv%d%d" % (c, b)], nvv[(c, b)])
             for e in range(2):
@@ -259,20 +304,18 @@ def rank_program(g, core, T, topo):
         ve.wait_ge(sem["mf%d" % c], 4)
         ve.tensor_copy(out=o[c][:, :], in_=pf[c][:, 0:256]).then_inc(sem["vf%d" % c], 1)
 
+    wait_weights(0, 1)
+    te.matmul(out=T.pw1[:, 0:128], lhsT=T.w0[:, 256:384], rhs=T.ident[:, :], start=True, stop=True).then_inc(sem.mt, 1)
+    ve.wait_ge(sem.mt, 1)
+    ve.tensor_copy(out=T.tb[:, :], in_=T.pw1[:, 0:128]).then_inc(sem.vt, 1)
+
     streams = [(c, b) for c in range(2) for b in range(2)]
-    mm_t(0)
-    ev_t(0)
-    for c, b in streams:
-        do_pass(0, c, b)
-    for q in range(1, n):
-        mm_p(q - 1)
-        if q < n - 1:
-            mm_t(q)
-        ev_p(q - 1)
-        if q < n - 1:
-            ev_t(q)
-            for c, b in streams:
-                do_pass(q, c, b)
+    for q in range(n - 1):
+        for c, b in streams[:3]:
+            do_pass(q, c, b)
+        if q != first:
+            do_p(q)
+        do_pass(q, *streams[3])
     for c in range(2):
         for b in range(2):
             do_pass(n - 1, c, b)

from concourse.bass import DstId, RemoteDMATransfer
from concourse.mybir import AluOpType

K = 4
BF = "bfloat16"
F32 = "float32"
SCRATCH = {
    "xs": ("dram", [8, 128, 256], BF),
    "ys": ("dram", [8, 128, 256], BF),
    "w0": ("sbuf", [128, 384], BF),
    "wb": ("sbuf", [128, 5 * 256], BF),
    "w2r": ("sbuf", [128, 128], BF),
    "tb": ("sbuf", [128, 128], BF),
    "pb": ("sbuf", [128, 5 * 128], BF),
    "ones": ("sbuf", [128, 128], BF), "ident": ("sbuf", [128, 128], BF),
    "xb": ("sbuf", [128, 512], BF),
    "u0": ("sbuf", [128, 256], BF), "u1": ("sbuf", [128, 256], BF),
    "v0": ("sbuf", [128, 256], BF), "v1": ("sbuf", [128, 256], BF),
    "o0": ("sbuf", [128, 256], BF), "o1": ("sbuf", [128, 256], BF),
    "zero": ("sbuf", [128, 128], BF),
    "ps00": ("psum", [128, 512], F32), "ps01": ("psum", [128, 512], F32),
    "ps10": ("psum", [128, 512], F32), "ps11": ("psum", [128, 512], F32),
    "pf0": ("psum", [128, 512], F32), "pf1": ("psum", [128, 512], F32),
    "pw0": ("psum", [128, 512], F32), "pw1": ("psum", [128, 512], F32),
}
SEMAPHORES = (["wl", "wl2", "xl0", "xl1", "sent", "st", "wr0", "wr1", "wn", "w0a", "xa0", "xa1", "zr", "zs", "idn",
               "mt", "vt", "mf0", "mf1", "vf0", "vf1"]
              + ["%s%d%d" % (a, c, b) for a in ("mm", "vv") for c in range(2) for b in range(2)]
              + ["%s%d" % (a, s) for s in range(1, 6) for a in ("ws", "wt", "wq", "wx", "wp", "wy")]
              + ["%s%d" % (a, s) for s in range(5) for a in ("mp", "vp")]
              + ["ya%d" % c for c in range(8)])


def _bits(mask):
    return [1 << i for i in range(mask.bit_length()) if (mask >> i) & 1]


def _split(mask, n):
    es = _bits(mask)
    per = len(es) // n
    return [sum(es[i * per:(i + 1) * per]) for i in range(n)]


def rank_program(g, core, T, topo):
    cores = list(T.cores)
    n = len(cores)
    src, snk = cores[0], cores[-1]
    sem = T.sem
    te, ve = g.tensor, g.vector
    allc = range(topo.CORES_PER_CHIP * topo.CHIPS)

    def on_chip(c):
        return [d for d in allc if topo.chip(d) == topo.chip(c) and d != c]

    def did(c):
        rid, pid, _ = topo.addr(c)
        return DstId(rid=rid, pnc=pid)

    comp = [c for c in on_chip(src) if topo.may_write(c, snk) and c not in cores][:K]
    direct = [s for s in range(1, n) if topo.may_write(cores[s], comp[0])]
    first = direct[0]
    scat = direct[1:]
    nxt = first + 1
    waves = [(s, p) for s in scat for p in range(2) if (s, p) != (nxt, 0)]
    relay = {}
    relays_of = {}
    for s in range(1, n):
        if s not in direct:
            rl = [c for c in on_chip(cores[s]) if topo.may_write(c, comp[0]) and c not in cores][:K]
            if s == n - 1:
                rl = [c for c in rl if topo.die(c) != topo.die(cores[direct[0]])]
            relays_of[s] = rl
            for i, c in enumerate(rl):
                relay[c] = (s, i)

    def blk(t, s):
        return t[:, s * 128:(s + 1) * 128]

    def quarter(s, part, j):
        return ((s - 1) * 256 + part * 128 + j * (128 // K), 128 // K,
                sem["%s%d" % (("wq", "wx")[part], s)], sem["%s%d" % (("wp", "wy")[part], s)])

    def make_identity():
        ve.memset(T.ones[:, :], 1.0).then_inc(sem.zs, 1)
        g.wait_ge(sem.zs, 1)
        g.affine_select(out=T.ident[:, :], in_=T.ones[:, :], pattern=[[-1, 128]], compare_op=AluOpType.is_equal,
                        fill=0.0, base=0, channel_multiplier=1).then_inc(sem.idn, 1)
        te.wait_ge(sem.idn, 1)

    rank = T.rank_of(core)
    sent = 0

    if core == src:
        g.sync.dma_start(T.w0[0:64, 0:256], T.w1[:, :]).then_inc(sem.wl, 16)
        g.scalar.dma_start(T.w0[64:128, 0:256], T.w1[:, :]).then_inc(sem.wl, 16)
        g.sync.dma_start(T.w0[:, 256:384], T.w2[:, :]).then_inc(sem.wl, 16)
        g.scalar.dma_start(T.xs[0:4], T.x[0:8]).then_inc(sem.xl0, 16)
        g.sync.dma_start(T.xs[4:8], T.x[8:16]).then_inc(sem.xl1, 16)
        es = _bits(topo.mask(src, comp[0]))
        near = [c for c in comp if topo.die(c) == topo.die(src)]
        far = [c for c in comp if topo.die(c) != topo.die(src)]
        ne = len(es) // K
        if len(near) == len(far):
            grp_of = {}
            for lst, mine in ((near, es[0::2]), (far, es[1::2])):
                for i, c in enumerate(lst):
                    grp_of[c] = sum(mine[i * ne:(i + 1) * ne])
            grp = [grp_of[c] for c in comp]
        else:
            grp = _split(topo.mask(src, comp[0]), K)
        g.wait_ge(sem.wl, 48)
        g.remote_dma_fused([RemoteDMATransfer(dst_ids=[did(c)], dma_engine_mask=grp[j], remote_sem=sem.w0a,
                                              src=T.w0[:, :], dst=T.w0[:, :]) for j, c in enumerate(comp)],
                           local_sem=sem.sent)
        sent += K * ne
        for h in range(2):
            g.wait_ge(sem["xl%d" % h], 16)
            g.remote_dma_fused([RemoteDMATransfer(dst_ids=[did(c)], dma_engine_mask=grp[j],
                                                  remote_sem=sem["xa%d" % h], src=T.xs[4 * h + j],
                                                  dst=T.xb[:, h * 256:(h + 1) * 256]) for j, c in enumerate(comp)],
                               local_sem=sem.sent)
            sent += K * ne
        g.wait_ge(sem.sent, sent)
        return

    if rank is not None:
        s = rank
        a0 = (s - 1) * 256
        turned = s < n - 1
        g.sync.dma_start(T.wb[:, a0:a0 + 128], T.w1[:, :]).then_inc(sem.wl, 16)
        if turned:
            g.scalar.dma_start(T.w2r[:, :], T.w2[:, :]).then_inc(sem.wl2, 16)
            make_identity()
            te.wait_ge(sem.wl2, 16)
            te.matmul(out=T.pw1[:, 0:128], lhsT=T.w2r[:, :], rhs=T.ident[:, :],
                      start=True, stop=True).then_inc(sem.mt, 1)
            ve.wait_ge(sem.mt, 1)
            ve.tensor_copy(out=T.wb[:, a0 + 128:a0 + 256], in_=T.pw1[:, 0:128]).then_inc(sem.vt, 1)
        else:
            g.scalar.dma_start(T.wb[:, a0 + 128:a0 + 256], T.w2[:, :]).then_inc(sem.wl2, 16)
        if s == first:
            te.wait_ge(sem.vt, 1)
            te.wait_ge(sem.wn, len(_bits(topo.mask(cores[nxt], core))))
            te.matmul(out=T.pw0[:, 0:128], lhsT=T.wb[:, a0 + 128:a0 + 256], rhs=T.wb[:, s * 256:s * 256 + 128],
                      start=True, stop=True).then_inc(sem["mp%d" % s], 1)
            ve.wait_ge(sem["mp%d" % s], 1)
            ve.tensor_copy(out=blk(T.pb, s), in_=T.pw0[:, 0:128]).then_inc(sem["vp%d" % s], 1)
        g.wait_ge(sem.wl, 16)
        for part in range(2):
            a = a0 + part * 128
            if part == 1:
                if s == first:
                    g.wait_ge(sem["vp%d" % s], 1)
                elif turned:
                    g.wait_ge(sem.vt, 1)
                else:
                    g.wait_ge(sem.wl2, 16)
            if (s, part) == (nxt, 0):
                m = topo.mask(core, cores[first])
                rid, pid, _ = topo.addr(cores[first])
                g.remote_dma(T.wb[:, a:a + 128], T.wb[:, a:a + 128], sem.wn, sem.sent, pid, rid, m)
                sent += len(_bits(m))
            elif s in direct:
                grp = _split(topo.mask(core, comp[0]), K)
                tr = []
                for j, c in enumerate(comp):
                    if s != first:
                        b, wd, rs, _ = quarter(s, part, j)
                        ap = T.wb[:, b:b + wd]
                    else:
                        rs = sem["%s%d" % (("ws", "wt")[part], s)]
                        ap = T.wb[:, a:a + 128] if part == 0 else blk(T.pb, s)
                    tr.append(RemoteDMATransfer(dst_ids=[did(c)], dma_engine_mask=grp[j], remote_sem=rs,
                                                src=ap, dst=ap))
                g.remote_dma_fused(tr, local_sem=sem.sent)
                sent += K * len(_bits(grp[0]))
            else:
                rl = relays_of[s]
                m = topo.mask(core, rl[0])
                g.remote_dma_fused([RemoteDMATransfer(dst_ids=[did(c) for c in rl], dma_engine_mask=m,
                                                      remote_sem=sem["wr%d" % part], srcs=[T.wb[:, a:a + 128]],
                                                      dsts=[T.wb[:, a:a + 128] for c in rl])], local_sem=sem.sent)
                sent += len(_bits(m))
        if core == snk:
            ne = len(_bits(topo.mask(comp[0], snk)))
            for h in range(2):
                for j in range(K):
                    c = 4 * h + j
                    q = g.sync if j % 2 == 0 else g.scalar
                    q.wait_ge(sem["ya%d" % c], ne)
                    q.dma_start(T.y[2 * c:2 * c + 2], T.ys[c]).then_inc(sem.st, 16)
            g.wait_ge(sem.st, 16 * 8)
        g.wait_ge(sem.sent, sent)
        return

    if core in relay:
        s, i = relay[core]
        mine = comp[i::len(relays_of[s])]
        m = topo.mask(core, comp[i])
        for part, nm in enumerate(("ws", "wt")):
            a = (s - 1) * 256 + part * 128
            g.wait_ge(sem["wr%d" % part], len(_bits(topo.mask(cores[s], core))))
            g.remote_dma_fused([RemoteDMATransfer(dst_ids=[did(c) for c in mine], dma_engine_mask=m,
                                                  remote_sem=sem["%s%d" % (nm, s)], srcs=[T.wb[:, a:a + 128]],
                                                  dsts=[T.wb[:, a:a + 128] for c in mine])], local_sem=sem.sent)
        g.wait_ge(sem.sent, 2 * len(_bits(m)))
        return

    if core not in comp:
        return

    j = comp.index(core)
    out_mask = topo.mask(core, snk)
    n_out = len(_bits(out_mask))
    peers = [c for c in comp if c != core]

    make_identity()
    ve.memset(T.zero[:, :], 0.0).then_inc(sem.zr, 1)
    ve.wait_ge(sem.zr, 1)

    nq = len(_bits(_split(topo.mask(cores[scat[0]], core), K)[0]))
    for s, part in waves:
        a, wd, s_in, s_on = quarter(s, part, j)
        g.wait_ge(s_in, nq)
        g.remote_dma_fused([RemoteDMATransfer(dst_ids=[did(c) for c in peers], dma_engine_mask=out_mask,
                                              remote_sem=s_on, srcs=[T.wb[:, a:a + wd]],
                                              dsts=[T.wb[:, a:a + wd] for c in peers])], local_sem=sem.sent)
        sent += n_out

    n_x = len(_bits(topo.mask(src, core))) // K
    ps = [[T.ps00, T.ps01], [T.ps10, T.ps11]]
    pf = [T.pf0, T.pf1]
    u = [T.u0, T.u1]
    v = [T.v0, T.v1]
    o = [T.o0, T.o1]
    nmm = {}
    nvv = {}
    seen = set()

    def wait_weights(s, part):
        key = (s, part) if s else s
        if key in seen:
            return
        seen.add(key)
        if s == 0:
            te.wait_ge(sem.w0a, n_x)
        elif key in waves:
            _, _, s_in, s_on = quarter(s, part, j)
            te.wait_ge(s_in, nq)
            te.wait_ge(s_on, n_out * len(peers))
        elif s in direct:
            te.wait_ge(sem["%s%d" % (("ws", "wt")[part], s)], len(_bits(_split(topo.mask(cores[s], core), K)[0])))
        else:
            te.wait_ge(sem["%s%d" % (("ws", "wt")[part], s)],
                       len(_bits(topo.mask(relays_of[s][j % len(relays_of[s])], core))))

    def do_p(s):
        wait_weights(s, 1)
        wait_weights(s + 1, 0)
        if s == 0:
            te.wait_ge(sem.vt, 1)
        te.matmul(out=T.pw0[:, 0:128], lhsT=T.tb[:, :] if s == 0 else T.wb[:, (s - 1) * 256 + 128:s * 256],
                  rhs=T.wb[:, s * 256:s * 256 + 128], start=True, stop=True).then_inc(sem["mp%d" % s], 1)
        ve.wait_ge(sem["mp%d" % s], 1)
        ve.tensor_copy(out=blk(T.pb, s), in_=T.pw0[:, 0:128]).then_inc(sem["vp%d" % s], 1)

    def do_pass(q, c, b):
        k = (c, b)
        mm, vv = sem["mm%d%d" % k], sem["vv%d%d" % k]
        bank = ps[c][b][:, 0:128]
        if q == 0:
            wait_weights(0, 0)
            te.wait_ge(sem["xa%d" % c], n_x)
            for e in range(2):
                te.matmul(out=bank, lhsT=T.w0[b * 64:(b + 1) * 64, e * 128:(e + 1) * 128],
                          rhs=T.xb[b * 64:(b + 1) * 64, c * 256 + e * 128:c * 256 + (e + 1) * 128],
                          start=(e == 0), stop=(e == 1)).then_inc(mm, 1)
            nmm[k] = 2
            nvv[k] = 0
        else:
            te.wait_ge(vv, nvv[k])
            if q - 1 == first:
                wait_weights(first, 1)
            else:
                te.wait_ge(sem["vp%d" % (q - 1)], 1)
            te.matmul(out=bank, lhsT=blk(T.pb, q - 1), rhs=blk(u[c] if q % 2 else v[c], b),
                      start=True, stop=True).then_inc(mm, 1)
            nmm[k] += 1
        ve.wait_ge(mm, nmm[k])
        ve.tensor_tensor(out=blk(v[c] if q % 2 else u[c], b), in0=bank, in1=T.zero[:, :],
                         op=AluOpType.max).then_inc(vv, 1)
        nvv[k] += 1

    def do_last(c):
        w0c = (n - 2) * 256 + 128
        h = u[c] if n % 2 else v[c]
        wait_weights(n - 1, 1)
        for b in range(2):
            te.wait_ge(sem["vv%d%d" % (c, b)], nvv[(c, b)])
            for e in range(2):
                te.matmul(out=pf[c][b * 64:(b + 1) * 64, e * 128:(e + 1) * 128],
                          lhsT=T.wb[:, w0c + e:w0c + 128:2], rhs=blk(h, b),
                          start=True, stop=True).then_inc(sem["mf%d" % c], 1)
        ve.wait_ge(sem["mf%d" % c], 4)
        ve.tensor_copy(out=o[c][:, :], in_=pf[c][:, 0:256]).then_inc(sem["vf%d" % c], 1)

    wait_weights(0, 1)
    te.matmul(out=T.pw1[:, 0:128], lhsT=T.w0[:, 256:384], rhs=T.ident[:, :], start=True, stop=True).then_inc(sem.mt, 1)
    ve.wait_ge(sem.mt, 1)
    ve.tensor_copy(out=T.tb[:, :], in_=T.pw1[:, 0:128]).then_inc(sem.vt, 1)

    streams = [(c, b) for c in range(2) for b in range(2)]
    for q in range(n - 1):
        for c, b in streams[:3]:
            do_pass(q, c, b)
        if q != first:
            do_p(q)
        do_pass(q, *streams[3])
    for c in range(2):
        for b in range(2):
            do_pass(n - 1, c, b)
        do_last(c)

    rid, pid, _ = topo.addr(snk)
    for c in range(2):
        g.wait_ge(sem["vf%d" % c], 1)
        g.remote_dma(T.ys[4 * c + j], o[c][:, :], sem["ya%d" % (4 * c + j)], sem.sent, pid, rid, out_mask)
        sent += n_out
    g.wait_ge(sem.sent, sent)
